import numpy as np
import ml_dtypes


def mxq(x, axis, fmt="e4m3"):
    dtype, down = {"e4m3": (ml_dtypes.float8_e4m3fn, 7), "e5m2": (ml_dtypes.float8_e5m2, 14)}[fmt]
    v = np.moveaxis(np.asarray(x, np.float32).astype(ml_dtypes.bfloat16).astype(np.float64), axis, -1)
    blocks = v.reshape(v.shape[:-1] + (-1, 32))
    amax = np.abs(blocks).max(-1, keepdims=True)
    byte = np.maximum(np.where(amax > 0, np.frexp(amax)[1] - 1 + 127, 0) - down, 1)
    scale = np.exp2(byte - 127.0)
    codes = (blocks / scale).astype(np.float32).astype(dtype).astype(np.float64)
    return np.moveaxis((codes * scale).reshape(v.shape), -1, axis)


WIDE = False


def mx_kscale(k):
    if not WIDE:
        return np.ones(k)
    levels = np.array([10, -10, 5, -5, 0])
    if k % 512:
        return np.exp2(np.random.permutation(np.resize(levels, k // 32))).repeat(32)
    a = np.empty((k // 512, 16))
    for p in range(k // 512):
        a[p, :8] = np.random.permutation(np.resize(levels, 8))
        for g in range(8):
            far = levels[np.abs(levels - a[p, g]) >= 10]
            a[p, g + 8] = far[np.random.randint(len(far))]
    return np.exp2(a.ravel()).repeat(32)


def f64(x):
    return np.asarray(x).astype(np.float64)


def striped(idx):
    return np.tile(idx.reshape(-1, 16).T, (8, 1)).astype(np.uint16)


def unstriped(offs):
    return offs[:16].T.reshape(-1).astype(np.int64)


E2M1 = np.array([0.0, 0.5, 1.0, 1.5, 2.0, 3.0, 4.0, 6.0, -0.0, -0.5, -1.0, -1.5, -2.0, -3.0, -4.0, -6.0])


def pack_weight(w, fmt):
    k, n = w.shape
    w = f64(np.asarray(w, np.float32).astype(ml_dtypes.bfloat16)).reshape(k // 32, 32, n)
    amax = np.abs(w).max(1)
    if fmt == "e4m3":
        byte = np.frexp(amax)[1] - 1 + 127 - 7
    else:
        mant, ex = np.frexp(amax / 6.0)
        byte = np.where(mant > 0.5, ex, ex - 1) + 127
    byte = np.clip(np.where(amax > 0, byte, 1), 1, 254)
    scaled = (w * np.exp2(127.0 - byte)[:, None, :]).reshape(k, n).astype(np.float32)
    by_word = np.ascontiguousarray(scaled.reshape(k // 512, 128, 4, n).transpose(0, 1, 3, 2))
    if fmt == "e4m3":
        words = by_word.astype(ml_dtypes.float8_e4m3fn).view(np.uint8)
    else:
        c = by_word.astype(ml_dtypes.float4_e2m1fn).view(np.uint8) & 0xF
        words = (c[..., 0::2] | (c[..., 1::2] << 4)).reshape(k // 512, 128, 2 * n)
    return np.ascontiguousarray(words), np.ascontiguousarray(byte.astype(np.uint8).reshape(k // 512, 16, n))


def unpack_weight(words, scales, fmt):
    g, _, n = scales.shape
    words = np.ascontiguousarray(words).reshape(g, 128, n, -1)
    if fmt == "e4m3":
        vals = words.view(ml_dtypes.float8_e4m3fn).astype(np.float64)
    else:
        nib = np.empty((g, 128, n, 4), np.uint8)
        nib[..., 0::2] = words & 0xF
        nib[..., 1::2] = words >> 4
        vals = E2M1[nib]
    vals = vals * np.repeat(np.exp2(scales.astype(np.float64) - 127.0), 8, axis=1)[..., None]
    return vals.transpose(0, 1, 3, 2).reshape(g * 512, n)


def gelu(v):
    return 0.5 * v * (1.0 + np.tanh(np.sqrt(2.0 / np.pi) * (v + 0.044715 * v**3)))


K, H, N, T, S, T2, P = 1024, 512, 768, 4096, 1024, 2048, 1024


def setup_inputs():
    n = np.random.standard_normal
    s = mx_kscale(K)[:, None]
    u = mx_kscale(H)[:, None]
    tab_words, tab_scales = pack_weight(n((K, T)) * s, "e4m3")
    w1 = (n((K, H)) / np.sqrt(K) / s * u.T).astype(np.float32)
    w2_words, w2_scales = pack_weight(n((K, H)) / np.sqrt(K) / s * u.T, "e2m1")
    w3 = (0.9 * n((K, N)) / np.sqrt(K) / s).astype(np.float32)
    w4_words, w4_scales = pack_weight(0.9 * n((H, N)) / np.sqrt(H) / u, "e2m1")
    page0 = (n((H, T2)) * u).astype(np.float32)
    base = (0.5 * n(N)).astype(np.float32)
    offs = striped(np.random.permutation(T)[:S])
    offs2 = striped(np.random.permutation(T2)[:S])
    offs3 = striped(np.random.permutation(T2)[:P])
    return {"tab_words": tab_words, "tab_scales": tab_scales, "w1": w1,
            "w2_words": w2_words, "w2_scales": w2_scales, "w3": w3,
            "w4_words": w4_words, "w4_scales": w4_scales, "page0": page0,
            "base": base, "offs": offs, "offs2": offs2, "offs3": offs3}


def reference(tab_words, tab_scales, w1, w2_words, w2_scales, w3, w4_words, w4_scales,
              page0, base, offs, offs2, offs3):
    v = unpack_weight(tab_words, tab_scales, "e4m3")[:, unstriped(offs)]
    w2 = unpack_weight(w2_words, w2_scales, "e2m1")
    w4 = unpack_weight(w4_words, w4_scales, "e2m1")
    surf = mxq(f64(w1), 0, "e4m3").T @ v
    hand = w2.T @ v
    page = f64(page0).copy()
    l2 = unstriped(offs2)
    page[:, l2] = page[:, l2] + np.maximum(surf, hand)
    x = mxq(page[:, unstriped(offs3)], 0, "e4m3")
    y = w4.T @ x + mxq(f64(w3), 0, "e4m3").T @ v
    return np.tanh(y + f64(base)[:, None])

@@ -1,0 +1,239 @@
+from contextlib import ExitStack
+
+import concourse.mybir as mybir
+
+K, H, N, T, S, T2, J = 1024, 512, 768, 4096, 1024, 2048, 1024
+FLOPS = 2 * S * (2 * K * H + K * N) + 2 * J * H * N
+
+F32 = mybir.dt.float32
+BF16 = mybir.dt.bfloat16
+I32 = mybir.dt.int32
+U32 = mybir.dt.uint32
+U16 = mybir.dt.uint16
+U8 = mybir.dt.uint8
+FP8X4 = mybir.dt.float8_e4m3fn_x4
+FP4X4 = mybir.dt.float4_e2m1fn_x4
+ALU = mybir.AluOpType
+ACT = mybir.ActivationFunctionType
+
+P = 128
+PACK = 4
+PASSES = K // (P * PACK)
+HALF = 512
+BANK = 512
+N_TILES = N // P
+KB = 1024
+CHUNKS = (256, 256, 256, 128, 128)
+SCALAR_WEAVES = 2
+
+
+def tile_list_kitchen_rating_scores_kernel(
+    tc, tab_words, tab_scales, w1, w2_words, w2_scales, w3, w4_words, w4_scales,
+    page0, base, offs, offs2, offs3, out,
+):
+    nc = tc.nc
+    with ExitStack() as ctx:
+        lists = ctx.enter_context(tc.tile_pool(name="lists", bufs=1))
+        keep = ctx.enter_context(tc.tile_pool(name="keep", bufs=1))
+        arena = ctx.enter_context(tc.tile_pool(name="arena", bufs=1))
+        psum = ctx.enter_context(tc.psum_pool(name="psum", bufs=8))
+
+        def placed(name, shape, dtype, offset):
+            return arena.tile(shape, dtype, name=name, offset=offset, align_bytes=64)
+
+        idx1 = lists.tile([P, S // 16], U16, name="idx1")
+        idx2 = lists.tile([P, S // 16], U16, name="idx2")
+        idx3 = lists.tile([P, J // 16], U16, name="idx3")
+
+        tab_s = placed("tab_s", [P, T], U8, 7 * KB)
+        tab_w = [placed("tab_w0", [P, T], I32, 57 * KB), placed("tab_w1", [P, T], I32, 9 * KB)]
+        w1_raw = [placed(f"w1_raw{a}", [P, PACK, H], F32, (25 + 8 * a) * KB) for a in range(PASSES)]
+        w1_b = [placed(f"w1_b{a}", [P, H * PACK], BF16, (45 + 4 * a) * KB) for a in range(PASSES)]
+        w3_raw = [placed(f"w3_raw{a}", [P, PACK, N], F32, (33 + 12 * a) * KB) for a in range(PASSES)]
+        page = [placed(f"page{t}", [P, T2], F32, at * KB) for t, at in enumerate((0, 25, 57, 9))]
+        w4_w = placed("w4_w", [P, 2 * N], U8, 65 * KB)
+        bias = placed("bias", [P, N_TILES], F32, 67 * KB)
+        w3_b = placed("w3_b", [P, PASSES * N * PACK], BF16, 73 * KB)
+        w2_raw = placed("w2_raw", [P, PASSES, 2 * H], U8, 71 * KB)
+        w2s_raw = keep.tile([P, PASSES, H], U8, name="w2s_raw", align_bytes=64)
+        w4_s = keep.tile([P, N], U8, name="w4_s", align_bytes=64)
+        v_s1 = keep.tile([P, S], U8, name="v_s1", align_bytes=64)
+
+        nc.vector.memset(tab_s[:].bitcast(I32), 0)
+        nc.vector.memset(v_s1[:].bitcast(I32), 0)
+        nc.gpsimd.memset(w2s_raw[:].rearrange("p a c -> p (a c)").bitcast(I32), 0)
+        nc.gpsimd.memset(w4_s[:].bitcast(I32), 0)
+
+        nc.sync.dma_start(idx1[:], offs)
+        nc.sync.dma_start(idx2[:], offs2)
+        nc.sync.dma_start(idx3[:], offs3)
+        ts_rows = tab_scales.rearrange("a (q r) t -> r q a t", r=4)
+        for r in range(4):
+            nc.scalar.dma_start(out=tab_s[r:P:16, :].bitcast(I32), in_=ts_rows[r].bitcast(I32))
+        nc.sync.dma_start(out=w2_raw[:].bitcast(I32), in_=w2_words.rearrange("a p c -> p a c").bitcast(I32))
+        for a in range(PASSES):
+            nc.sync.dma_start(out=w1_raw[a][:], in_=w1[a * 512:(a + 1) * 512, :].rearrange("(p j) c -> p j c", j=PACK))
+        for q in range(4):
+            nc.gpsimd.dma_start(
+                out=w2s_raw[32 * q:32 * q + 4].bitcast(I32),
+                in_=w2_scales[:, 4 * q:4 * q + 4, :].rearrange("a r c -> r a c").bitcast(I32))
+        for q in range(4):
+            nc.gpsimd.dma_start(out=w4_s[32 * q:32 * q + 4, :].bitcast(I32), in_=w4_scales[0, 4 * q:4 * q + 4, :].bitcast(I32))
+
+        def load_table(a):
+            nc.sync.dma_start(out=tab_w[a][:], in_=tab_words[a].rearrange("p t i -> p (t i)").bitcast(I32))
+
+        page_rows = page0.rearrange("(p t) c -> t p c", t=PACK)
+
+        def load_page(t):
+            nc.sync.dma_start(out=page[t][:], in_=page_rows[t])
+
+        w2_w = keep.tile([P, PASSES, 2 * H], U8, name="w2_w", align_bytes=64)
+        nc.vector.tensor_copy(
+            out=w2_w[:].bitcast(U16).rearrange("p a (t m) -> p a m t", t=PACK),
+            in_=w2_raw[:].bitcast(U16).rearrange("p a (m t) -> p a m t", t=PACK))
+        load_table(0)
+
+        v_s0 = keep.tile([P, S], U8, name="v_s0", align_bytes=64)
+        nc.vector.tensor_copy(v_s0[:], tab_s[:].indirect(idx1[:]))
+        nc.sync.dma_start(out=v_s1[0:112, :].bitcast(I32), in_=v_s0[16:128, :].bitcast(I32))
+        v_s = [v_s0, v_s1]
+        load_table(1)
+        load_page(0)
+
+        w2_s = placed("w2_s", [P, PASSES, H], U8, 8 * KB)
+        nc.vector.tensor_copy(
+            out=w2_s[:].rearrange("p a (t m) -> p a m t", t=PACK),
+            in_=w2s_raw[:].rearrange("p a (m t) -> p a m t", t=PACK))
+
+        w1_q, w1_s = [], []
+        for a in range(PASSES):
+            nc.scalar.copy(
+                out=w1_b[a][:].rearrange("p (t m j) -> p m t j", t=PACK, j=PACK),
+                in_=w1_raw[a][:].rearrange("p j (m t) -> p m t j", t=PACK))
+            codes = keep.tile([P, H], U32, name=f"w1_q{a}", align_bytes=64)
+            scales = keep.tile([P, H], U8, name=f"w1_s{a}", align_bytes=64)
+            nc.vector.quantize_mx(out=codes[:].bitcast(FP8X4), scales=scales[:], in_=w1_b[a][:])
+            w1_q.append(codes)
+            w1_s.append(scales)
+        load_page(1)
+        for a in range(PASSES):
+            nc.sync.dma_start(out=w3_raw[a][:], in_=w3[a * 512:(a + 1) * 512, :].rearrange("(p j) c -> p j c", j=PACK))
+
+        v_w = {}
+        for a in range(PASSES):
+            for u in range(2):
+                words = keep.tile([P, HALF], U32, name=f"v_w{a}{u}", align_bytes=64)
+                nc.vector.tensor_copy(words[:], tab_w[a][:].bitcast(U32).indirect(idx1[:, 32 * u:32 * (u + 1)]))
+                v_w[a, u] = words
+        load_page(2)
+        nc.sync.dma_start(out=w4_w[:].bitcast(I32), in_=w4_words[0].bitcast(I32))
+        with nc.allow_non_contiguous_dma(reason="one bias value for each partition and output tile"):
+            nc.sync.dma_start(out=bias[:], in_=base.rearrange("(c p) -> p c", p=P))
+        load_page(3)
+
+        def v_cols(a, j0, n):
+            u, c = divmod(j0, HALF)
+            return v_w[a, u][:, c:c + n].bitcast(FP8X4), v_s[a][:, j0:j0 + n]
+
+        w3_q = keep.tile([P, PASSES * N], U32, name="w3_q", align_bytes=64)
+        w3_s = keep.tile([P, PASSES * N], U8, name="w3_s", align_bytes=64)
+
+        def w3_prepare():
+            for a in range(PASSES):
+                for u in range(2):
+                    c0 = u * (N // 2)
+                    o0 = (a * N + c0) * PACK
+                    nc.scalar.copy(
+                        out=w3_b[:, o0:o0 + N // 2 * PACK].rearrange("p (c i j) -> p c j i", i=4, j=PACK),
+                        in_=w3_raw[a][:, :, c0:c0 + N // 2].rearrange("p j (c i) -> p c j i", i=4))
+            for c0, c1 in ((0, 1024), (1024, 1536)):
+                nc.vector.quantize_mx(out=w3_q[:, c0:c1].bitcast(FP8X4), scales=w3_s[:, c0:c1], in_=w3_b[:, 4 * c0:4 * c1])
+
+        h = [keep.tile([P, S], F32, name=f"h{t}") for t in range(PACK)]
+
+        def product(codes, scales, t, u):
+            acc = psum.tile([P, HALF], F32, name="bank")
+            for a in range(PASSES):
+                rhs, rhs_s = v_cols(a, u * HALF, HALF)
+                nc.tensor.matmul_mx(out=acc[:], lhsT=codes(a, t), lhsT_scale=scales(a, t),
+                                    rhs=rhs, rhs_scale=rhs_s, start=(a == 0), stop=(a == PASSES - 1))
+            return acc
+
+        def hand(t, u):
+            acc = product(lambda a, t: w2_w[:, a, 2 * t * P:2 * (t + 1) * P].bitcast(FP4X4),
+                          lambda a, t: w2_s[:, a, t * P:(t + 1) * P], t, u)
+            nc.scalar.copy(out=h[t][:, u * HALF:(u + 1) * HALF], in_=acc[:])
+
+        def surf(t, u):
+            acc = product(lambda a, t: w1_q[a][:, t * P:(t + 1) * P].bitcast(FP8X4),
+                          lambda a, t: w1_s[a][:, t * P:(t + 1) * P], t, u)
+            js = slice(u * HALF, (u + 1) * HALF)
+            nc.vector.tensor_tensor(out=h[t][:, js], in0=acc[:], in1=h[t][:, js], op=ALU.max)
+
+        for u in range(2):
+            hand(0, u)
+            surf(0, u)
+        for t in range(1, PACK):
+            for u in range(2):
+                hand(t, u)
+        for t in range(1, PACK):
+            for u in range(2):
+                surf(t, u)
+        for t in range(PACK):
+            if t == PACK - 1:
+                w3_prepare()
+                old = placed(f"old{t}", [P, S], F32, 73 * KB)
+            else:
+                old = keep.tile([P, S], F32, name=f"old{t}")
+            nc.vector.tensor_copy(old[:], page[t][:].indirect(idx2[:]))
+            nc.vector.tensor_tensor(page[t][:].indirect(idx2[:]), old[:], h[t][:], ALU.add)
+
+        starts = [sum(CHUNKS[:c]) for c in range(len(CHUNKS))]
+        per_bank = {256: 2, 128: 3}
+        todo = [(c, g0) for c, n in enumerate(CHUNKS) for g0 in range(0, N_TILES, per_bank[n])]
+        banks = {}
+
+        def w3_passes(c, g0):
+            n = CHUNKS[c]
+            acc = psum.tile([P, per_bank[n], n], F32, name="bank")
+            banks[c, g0] = acc
+            for e in range(per_bank[n]):
+                for a in range(PASSES):
+                    n0 = a * N + (g0 + e) * P
+                    rhs, rhs_s = v_cols(a, starts[c], n)
+                    nc.tensor.matmul_mx(
+                        out=acc[:, e, :], lhsT=w3_q[:, n0:n0 + P].bitcast(FP8X4), lhsT_scale=w3_s[:, n0:n0 + P],
+                        rhs=rhs, rhs_scale=rhs_s, start=(e == 0 and a == 0), stop=False)
+
+        for c, g0 in todo[:8]:
+            w3_passes(c, g0)
+        out_view = out.rearrange("(g p) j -> p g j", p=P)
+        x_at = [77 * KB + 8 * j0 for j0 in starts]
+        for c, n in enumerate(CHUNKS):
+            j0 = starts[c]
+            picked = placed(f"picked{c}", [P, PACK, n], BF16, (73 + 2 * c) * KB if c < 2 else x_at[c - 2])
+            for t in range(PACK):
+                nc.vector.tensor_copy(picked[:, t, :], page[t][:].indirect(idx3[:, j0 // 16:(j0 + n) // 16]))
+            x_b = placed(f"x_b{c}", [P, n * PACK], BF16, x_at[c])
+            weave = nc.scalar.copy if c < SCALAR_WEAVES else nc.vector.tensor_copy
+            weave(out=x_b[:].rearrange("p (c i t) -> p c t i", i=4, t=PACK),
+                  in_=picked[:].rearrange("p t (c i) -> p c t i", i=4))
+            x_q = keep.tile([P, n], U32, name=f"x_q{c}", align_bytes=64)
+            x_s = keep.tile([P, n], U8, name=f"x_s{c}", align_bytes=64)
+            nc.vector.quantize_mx(out=x_q[:].bitcast(FP8X4), scales=x_s[:], in_=x_b[:])
+            for g0 in range(0, N_TILES, per_bank[n]):
+                acc = banks[c, g0]
+                res = placed(f"res{c}_{g0}", [P, per_bank[n], n], F32, 33 * KB + 4 * (N_TILES * j0 + g0 * n))
+                for e in range(per_bank[n]):
+                    n0 = (g0 + e) * P
+                    nc.tensor.matmul_mx(
+                        out=acc[:, e, :], lhsT=w4_w[:, 2 * n0:2 * (n0 + P)].bitcast(FP4X4), lhsT_scale=w4_s[:, n0:n0 + P],
+                        rhs=x_q[:].bitcast(FP8X4), rhs_scale=x_s[:], start=False, stop=(e == per_bank[n] - 1))
+                for e in range(per_bank[n]):
+                    g = g0 + e
+                    nc.scalar.activation(out=res[:, e, :], in_=acc[:, e, :], func=ACT.Tanh, bias=bias[:, g:g + 1])
+                nc.sync.dma_start(out=out_view[:, g0:g0 + per_bank[n], j0:j0 + n], in_=res[:])
+                nxt = todo.index((c, g0)) + 8
+                if nxt < len(todo):
+                    w3_passes(*todo[nxt])

@@ -186,8 +186,12 @@ def tile_list_kitchen_rating_scores_kernel(
                 old = placed(f"old{t}", [P, S], F32, 73 * KB)
             else:
                 old = keep.tile([P, S], F32, name=f"old{t}")
-            nc.vector.tensor_copy(old[:], page[t][:].indirect(idx2[:]))
-            nc.vector.tensor_tensor(page[t][:].indirect(idx2[:]), old[:], h[t][:], ALU.add)
+            if t == 0:
+                nc.vector.tensor_copy(old[:], page[t][:].indirect(idx2[:]))
+                nc.vector.tensor_tensor(page[t][:].indirect(idx2[:]), old[:], h[t][:], ALU.add)
+            else:
+                nc.vector.tensor_tensor(old[:], page[t][:].indirect(idx2[:]), h[t][:], ALU.add)
+                nc.vector.tensor_copy(page[t][:].indirect(idx2[:]), old[:])
 
         starts = [sum(CHUNKS[:c]) for c in range(len(CHUNKS))]
         per_bank = {256: 2, 128: 3}

from contextlib import ExitStack

import concourse.mybir as mybir

K, H, N, T, S, T2, J = 1024, 512, 768, 4096, 1024, 2048, 1024
FLOPS = 2 * S * (2 * K * H + K * N) + 2 * J * H * N

F32 = mybir.dt.float32
BF16 = mybir.dt.bfloat16
I32 = mybir.dt.int32
U32 = mybir.dt.uint32
U16 = mybir.dt.uint16
U8 = mybir.dt.uint8
FP8X4 = mybir.dt.float8_e4m3fn_x4
FP4X4 = mybir.dt.float4_e2m1fn_x4
ALU = mybir.AluOpType
ACT = mybir.ActivationFunctionType

P = 128
PACK = 4
PASSES = K // (P * PACK)
HALF = 512
BANK = 512
N_TILES = N // P
KB = 1024
CHUNKS = (256, 256, 256, 128, 128)
SCALAR_WEAVES = 2


def tile_list_kitchen_rating_scores_kernel(
    tc, tab_words, tab_scales, w1, w2_words, w2_scales, w3, w4_words, w4_scales,
    page0, base, offs, offs2, offs3, out,
):
    nc = tc.nc
    with ExitStack() as ctx:
        lists = ctx.enter_context(tc.tile_pool(name="lists", bufs=1))
        keep = ctx.enter_context(tc.tile_pool(name="keep", bufs=1))
        arena = ctx.enter_context(tc.tile_pool(name="arena", bufs=1))
        psum = ctx.enter_context(tc.psum_pool(name="psum", bufs=8))

        def placed(name, shape, dtype, offset):
            return arena.tile(shape, dtype, name=name, offset=offset, align_bytes=64)

        idx1 = lists.tile([P, S // 16], U16, name="idx1")
        idx2 = lists.tile([P, S // 16], U16, name="idx2")
        idx3 = lists.tile([P, J // 16], U16, name="idx3")

        tab_s = placed("tab_s", [P, T], U8, 7 * KB)
        tab_w = [placed("tab_w0", [P, T], I32, 57 * KB), placed("tab_w1", [P, T], I32, 9 * KB)]
        w1_raw = [placed(f"w1_raw{a}", [P, PACK, H], F32, (25 + 8 * a) * KB) for a in range(PASSES)]
        w1_b = [placed(f"w1_b{a}", [P, H * PACK], BF16, (45 + 4 * a) * KB) for a in range(PASSES)]
        w3_raw = [placed(f"w3_raw{a}", [P, PACK, N], F32, (33 + 12 * a) * KB) for a in range(PASSES)]
        page = [placed(f"page{t}", [P, T2], F32, at * KB) for t, at in enumerate((0, 25, 57, 9))]
        w4_w = placed("w4_w", [P, 2 * N], U8, 65 * KB)
        bias = placed("bias", [P, N_TILES], F32, 67 * KB)
        w3_b = placed("w3_b", [P, PASSES * N * PACK], BF16, 73 * KB)
        w2_raw = placed("w2_raw", [P, PASSES, 2 * H], U8, 71 * KB)
        w2s_raw = keep.tile([P, PASSES, H], U8, name="w2s_raw", align_bytes=64)
        w4_s = keep.tile([P, N], U8, name="w4_s", align_bytes=64)
        v_s1 = keep.tile([P, S], U8, name="v_s1", align_bytes=64)

        nc.vector.memset(tab_s[:].bitcast(I32), 0)
        nc.vector.memset(v_s1[:].bitcast(I32), 0)
        nc.gpsimd.memset(w2s_raw[:].rearrange("p a c -> p (a c)").bitcast(I32), 0)
        nc.gpsimd.memset(w4_s[:].bitcast(I32), 0)

        nc.sync.dma_start(idx1[:], offs)
        nc.sync.dma_start(idx2[:], offs2)
        nc.sync.dma_start(idx3[:], offs3)
        ts_rows = tab_scales.rearrange("a (q r) t -> r q a t", r=4)
        for r in range(4):
            nc.scalar.dma_start(out=tab_s[r:P:16, :].bitcast(I32), in_=ts_rows[r].bitcast(I32))
        nc.sync.dma_start(out=w2_raw[:].bitcast(I32), in_=w2_words.rearrange("a p c -> p a c").bitcast(I32))
        for a in range(PASSES):
            nc.sync.dma_start(out=w1_raw[a][:], in_=w1[a * 512:(a + 1) * 512, :].rearrange("(p j) c -> p j c", j=PACK))
        for q in range(4):
            nc.gpsimd.dma_start(
                out=w2s_raw[32 * q:32 * q + 4].bitcast(I32),
                in_=w2_scales[:, 4 * q:4 * q + 4, :].rearrange("a r c -> r a c").bitcast(I32))
        for q in range(4):
            nc.gpsimd.dma_start(out=w4_s[32 * q:32 * q + 4, :].bitcast(I32), in_=w4_scales[0, 4 * q:4 * q + 4, :].bitcast(I32))

        def load_table(a):
            nc.sync.dma_start(out=tab_w[a][:], in_=tab_words[a].rearrange("p t i -> p (t i)").bitcast(I32))

        page_rows = page0.rearrange("(p t) c -> t p c", t=PACK)

        def load_page(t):
            nc.sync.dma_start(out=page[t][:], in_=page_rows[t])

        w2_w = keep.tile([P, PASSES, 2 * H], U8, name="w2_w", align_bytes=64)
        nc.vector.tensor_copy(
            out=w2_w[:].bitcast(U16).rearrange("p a (t m) -> p a m t", t=PACK),
            in_=w2_raw[:].bitcast(U16).rearrange("p a (m t) -> p a m t", t=PACK))
        load_table(0)

        v_s0 = keep.tile([P, S], U8, name="v_s0", align_bytes=64)
        nc.vector.tensor_copy(v_s0[:], tab_s[:].indirect(idx1[:]))
        nc.sync.dma_start(out=v_s1[0:112, :].bitcast(I32), in_=v_s0[16:128, :].bitcast(I32))
        v_s = [v_s0, v_s1]
        load_table(1)
        load_page(0)

        w2_s = placed("w2_s", [P, PASSES, H], U8, 8 * KB)
        nc.vector.tensor_copy(
            out=w2_s[:].rearrange("p a (t m) -> p a m t", t=PACK),
            in_=w2s_raw[:].rearrange("p a (m t) -> p a m t", t=PACK))

        w1_q, w1_s = [], []
        for a in range(PASSES):
            nc.scalar.copy(
                out=w1_b[a][:].rearrange("p (t m j) -> p m t j", t=PACK, j=PACK),
                in_=w1_raw[a][:].rearrange("p j (m t) -> p m t j", t=PACK))
            codes = keep.tile([P, H], U32, name=f"w1_q{a}", align_bytes=64)
            scales = keep.tile([P, H], U8, name=f"w1_s{a}", align_bytes=64)
            nc.vector.quantize_mx(out=codes[:].bitcast(FP8X4), scales=scales[:], in_=w1_b[a][:])
            w1_q.append(codes)
            w1_s.append(scales)
        load_page(1)
        for a in range(PASSES):
            nc.sync.dma_start(out=w3_raw[a][:], in_=w3[a * 512:(a + 1) * 512, :].rearrange("(p j) c -> p j c", j=PACK))

        v_w = {}
        for a in range(PASSES):
            for u in range(2):
                words = keep.tile([P, HALF], U32, name=f"v_w{a}{u}", align_bytes=64)
                nc.vector.tensor_copy(words[:], tab_w[a][:].bitcast(U32).indirect(idx1[:, 32 * u:32 * (u + 1)]))
                v_w[a, u] = words
        load_page(2)
        nc.sync.dma_start(out=w4_w[:].bitcast(I32), in_=w4_words[0].bitcast(I32))
        with nc.allow_non_contiguous_dma(reason="one bias value for each partition and output tile"):
            nc.sync.dma_start(out=bias[:], in_=base.rearrange("(c p) -> p c", p=P))
        load_page(3)

        def v_cols(a, j0, n):
            u, c = divmod(j0, HALF)
            return v_w[a, u][:, c:c + n].bitcast(FP8X4), v_s[a][:, j0:j0 + n]

        w3_q = keep.tile([P, PASSES * N], U32, name="w3_q", align_bytes=64)
        w3_s = keep.tile([P, PASSES * N], U8, name="w3_s", align_bytes=64)

        def w3_prepare():
            for a in range(PASSES):
                for u in range(2):
                    c0 = u * (N // 2)
                    o0 = (a * N + c0) * PACK
                    nc.scalar.copy(
                        out=w3_b[:, o0:o0 + N // 2 * PACK].rearrange("p (c i j) -> p c j i", i=4, j=PACK),
                        in_=w3_raw[a][:, :, c0:c0 + N // 2].rearrange("p j (c i) -> p c j i", i=4))
            for c0, c1 in ((0, 1024), (1024, 1536)):
                nc.vector.quantize_mx(out=w3_q[:, c0:c1].bitcast(FP8X4), scales=w3_s[:, c0:c1], in_=w3_b[:, 4 * c0:4 * c1])

        h = [keep.tile([P, S], F32, name=f"h{t}") for t in range(PACK)]

        def product(codes, scales, t, u):
            acc = psum.tile([P, HALF], F32, name="bank")
            for a in range(PASSES):
                rhs, rhs_s = v_cols(a, u * HALF, HALF)
                nc.tensor.matmul_mx(out=acc[:], lhsT=codes(a, t), lhsT_scale=scales(a, t),
                                    rhs=rhs, rhs_scale=rhs_s, start=(a == 0), stop=(a == PASSES - 1))
            return acc

        def hand(t, u):
            acc = product(lambda a, t: w2_w[:, a, 2 * t * P:2 * (t + 1) * P].bitcast(FP4X4),
                          lambda a, t: w2_s[:, a, t * P:(t + 1) * P], t, u)
            nc.scalar.copy(out=h[t][:, u * HALF:(u + 1) * HALF], in_=acc[:])

        def surf(t, u):
            acc = product(lambda a, t: w1_q[a][:, t * P:(t + 1) * P].bitcast(FP8X4),
                          lambda a, t: w1_s[a][:, t * P:(t + 1) * P], t, u)
            js = slice(u * HALF, (u + 1) * HALF)
            nc.vector.tensor_tensor(out=h[t][:, js], in0=acc[:], in1=h[t][:, js], op=ALU.max)

        for u in range(2):
            hand(0, u)
            surf(0, u)
        for t in range(1, PACK):
            for u in range(2):
                hand(t, u)
        for t in range(1, PACK):
            for u in range(2):
                surf(t, u)
        for t in range(PACK):
            if t == PACK - 1:
                w3_prepare()
                old = placed(f"old{t}", [P, S], F32, 73 * KB)
            else:
                old = keep.tile([P, S], F32, name=f"old{t}")
            if t == 0:
                nc.vector.tensor_copy(old[:], page[t][:].indirect(idx2[:]))
                nc.vector.tensor_tensor(page[t][:].indirect(idx2[:]), old[:], h[t][:], ALU.add)
            else:
                nc.vector.tensor_tensor(old[:], page[t][:].indirect(idx2[:]), h[t][:], ALU.add)
                nc.vector.tensor_copy(page[t][:].indirect(idx2[:]), old[:])

        starts = [sum(CHUNKS[:c]) for c in range(len(CHUNKS))]
        per_bank = {256: 2, 128: 3}
        todo = [(c, g0) for c, n in enumerate(CHUNKS) for g0 in range(0, N_TILES, per_bank[n])]
        banks = {}

        def w3_passes(c, g0):
            n = CHUNKS[c]
            acc = psum.tile([P, per_bank[n], n], F32, name="bank")
            banks[c, g0] = acc
            for e in range(per_bank[n]):
                for a in range(PASSES):
                    n0 = a * N + (g0 + e) * P
                    rhs, rhs_s = v_cols(a, starts[c], n)
                    nc.tensor.matmul_mx(
                        out=acc[:, e, :], lhsT=w3_q[:, n0:n0 + P].bitcast(FP8X4), lhsT_scale=w3_s[:, n0:n0 + P],
                        rhs=rhs, rhs_scale=rhs_s, start=(e == 0 and a == 0), stop=False)

        for c, g0 in todo[:8]:
            w3_passes(c, g0)
        out_view = out.rearrange("(g p) j -> p g j", p=P)
        x_at = [77 * KB + 8 * j0 for j0 in starts]
        for c, n in enumerate(CHUNKS):
            j0 = starts[c]
            picked = placed(f"picked{c}", [P, PACK, n], BF16, (73 + 2 * c) * KB if c < 2 else x_at[c - 2])
            for t in range(PACK):
                nc.vector.tensor_copy(picked[:, t, :], page[t][:].indirect(idx3[:, j0 // 16:(j0 + n) // 16]))
            x_b = placed(f"x_b{c}", [P, n * PACK], BF16, x_at[c])
            weave = nc.scalar.copy if c < SCALAR_WEAVES else nc.vector.tensor_copy
            weave(out=x_b[:].rearrange("p (c i t) -> p c t i", i=4, t=PACK),
                  in_=picked[:].rearrange("p t (c i) -> p c t i", i=4))
            x_q = keep.tile([P, n], U32, name=f"x_q{c}", align_bytes=64)
            x_s = keep.tile([P, n], U8, name=f"x_s{c}", align_bytes=64)
            nc.vector.quantize_mx(out=x_q[:].bitcast(FP8X4), scales=x_s[:], in_=x_b[:])
            for g0 in range(0, N_TILES, per_bank[n]):
                acc = banks[c, g0]
                res = placed(f"res{c}_{g0}", [P, per_bank[n], n], F32, 33 * KB + 4 * (N_TILES * j0 + g0 * n))
                for e in range(per_bank[n]):
                    n0 = (g0 + e) * P
                    nc.tensor.matmul_mx(
                        out=acc[:, e, :], lhsT=w4_w[:, 2 * n0:2 * (n0 + P)].bitcast(FP4X4), lhsT_scale=w4_s[:, n0:n0 + P],
                        rhs=x_q[:].bitcast(FP8X4), rhs_scale=x_s[:], start=False, stop=(e == per_bank[n] - 1))
                for e in range(per_bank[n]):
                    g = g0 + e
                    nc.scalar.activation(out=res[:, e, :], in_=acc[:, e, :], func=ACT.Tanh, bias=bias[:, g:g + 1])
                nc.sync.dma_start(out=out_view[:, g0:g0 + per_bank[n], j0:j0 + n], in_=res[:])
                nxt = todo.index((c, g0)) + 8
                if nxt < len(todo):
                    w3_passes(*todo[nxt])
